import numpy as np
import ml_dtypes


def mxq(x, axis, fmt="e4m3"):
    dtype, down = {"e4m3": (ml_dtypes.float8_e4m3fn, 7), "e5m2": (ml_dtypes.float8_e5m2, 14)}[fmt]
    v = np.moveaxis(np.asarray(x, np.float32).astype(ml_dtypes.bfloat16).astype(np.float64), axis, -1)
    blocks = v.reshape(v.shape[:-1] + (-1, 32))
    amax = np.abs(blocks).max(-1, keepdims=True)
    byte = np.maximum(np.where(amax > 0, np.frexp(amax)[1] - 1 + 127, 0) - down, 1)
    scale = np.exp2(byte - 127.0)
    codes = (blocks / scale).astype(np.float32).astype(dtype).astype(np.float64)
    return np.moveaxis((codes * scale).reshape(v.shape), -1, axis)


WIDE = False


def mx_kscale(k):
    if not WIDE:
        return np.ones(k)
    levels = np.array([10, -10, 5, -5, 0])
    if k % 512:
        return np.exp2(np.random.permutation(np.resize(levels, k // 32))).repeat(32)
    a = np.empty((k // 512, 16))
    for p in range(k // 512):
        a[p, :8] = np.random.permutation(np.resize(levels, 8))
        for g in range(8):
            far = levels[np.abs(levels - a[p, g]) >= 10]
            a[p, g + 8] = far[np.random.randint(len(far))]
    return np.exp2(a.ravel()).repeat(32)


def f64(x):
    return np.asarray(x).astype(np.float64)


def striped(idx):
    return np.tile(idx.reshape(-1, 16).T, (8, 1)).astype(np.uint16)


def unstriped(offs):
    return offs[:16].T.reshape(-1).astype(np.int64)


def striped8(idx):
    return np.concatenate([x.reshape(-1, 16).T for x in idx]).astype(np.uint16)


def runs(offs, k):
    lists = np.stack([offs[16 * r : 16 * r + 16].T.reshape(-1) for r in range(8)]).astype(np.int64)
    return lists[np.arange(k) % 512 // 64]


def pack_weight(w):
    k, n = w.shape
    w = f64(np.asarray(w, np.float32).astype(ml_dtypes.bfloat16)).reshape(k // 32, 32, n)
    amax = np.abs(w).max(1)
    byte = np.clip(np.where(amax > 0, np.frexp(amax)[1] - 1 + 127 - 7, 1), 1, 254)
    scaled = (w * np.exp2(127.0 - byte)[:, None, :]).reshape(k, n).astype(np.float32)
    words = np.ascontiguousarray(scaled.reshape(k // 512, 128, 4, n).transpose(0, 1, 3, 2)).astype(ml_dtypes.float8_e4m3fn).view(np.uint8)
    return words, np.ascontiguousarray(byte.astype(np.uint8).reshape(k // 512, 16, n))


def unpack_weight(words, scales):
    g, p, n, _ = words.shape
    vals = np.ascontiguousarray(words).view(ml_dtypes.float8_e4m3fn).astype(np.float64) * np.repeat(np.exp2(scales.astype(np.float64) - 127.0), 8, axis=1)[..., None]
    return vals.transpose(0, 1, 3, 2).reshape(g * 512, n)

def planes(y):
    n, m = y.shape
    v = y.astype(np.float32).astype(ml_dtypes.bfloat16).astype(np.float64).reshape(n // 32, 32, m)
    top = np.abs(v).max(1)
    byte = np.clip(np.where(top > 0, np.frexp(top)[1] - 1 + 127 - 7, 1), 1, 254)
    codes = (v * np.exp2(127.0 - byte)[:, None, :]).reshape(n, m).astype(np.float32).astype(ml_dtypes.float8_e4m3fn).view(np.uint8)
    words = codes.reshape(n // 512, 128, 4, m).transpose(0, 1, 3, 2)
    return np.ascontiguousarray(words), np.ascontiguousarray(byte.astype(np.uint8).reshape(n // 512, 16, m))


K, T, S, H, C, U = 512, 2048, 512, 512, 512, 1024


def setup_inputs():
    n = np.random.standard_normal
    s = mx_kscale(K)[:, None]
    packed_xT = pack_weight(n((K, T)) * s)
    packed_w1 = pack_weight(n((K, H)) / np.sqrt(K) / s)
    packed_w2 = pack_weight(n((K, H)) / np.sqrt(K) / s)
    return {
        "x_words": packed_xT[0],
        "x_scales": packed_xT[1],
        "w1_words": packed_w1[0],
        "w1_scales": packed_w1[1],
        "w2_words": packed_w2[0],
        "w2_scales": packed_w2[1],
        "gs": (np.random.uniform(0.5, 1.5, (K, 1)) / s).astype(np.float32),
        "mem": n((C, U)).astype(np.float32),
        "offs": striped(np.random.permutation(T)[:S]),
        "two": striped(np.random.permutation(T)[:S]),
        "n1": striped8(np.stack([np.random.permutation(S) for _ in range(8)])),
        "n2": striped8(np.stack([np.random.permutation(S) for _ in range(8)])),
        "cand": striped(np.random.permutation(T)[:C]),
        "n3": striped8(np.stack([np.random.permutation(U)[:S] for _ in range(8)])),
    }


def reference(x_words, x_scales, w1_words, w1_scales, w2_words, w2_scales, gs, mem, offs, two, n1, n2, cand, n3):
    x_cand = unpack_weight(x_words, x_scales)[:, unstriped(cand)]
    xq = unpack_weight(x_words, x_scales)[:, unstriped(offs)]
    y = unpack_weight(w1_words, w1_scales).T @ xq
    x_two = unpack_weight(x_words, x_scales)[:, unstriped(two)]
    d = unpack_weight(w2_words, w2_scales).T @ x_two
    z = f64(gs) * (np.maximum(y, d[np.arange(H)[:, None], runs(n2, H)]) - (np.minimum(y[np.arange(H)[:, None], runs(n1, H)], d)))
    s = 0.0625 * ((x_cand.T @ mxq(z, 0, "e4m3")))
    out = f64(mem).copy()
    out[np.arange(C)[:, None], runs(n3, C)] = s
    return (out,) + planes(out)

@@ -1,0 +1,252 @@
+from contextlib import ExitStack
+
+import concourse.mybir as mybir
+
+F32 = mybir.dt.float32
+BF16 = mybir.dt.bfloat16
+I32 = mybir.dt.int32
+U32 = mybir.dt.uint32
+U16 = mybir.dt.uint16
+U8 = mybir.dt.uint8
+FP8X4 = mybir.dt.float8_e4m3fn_x4
+ALU = mybir.AluOpType
+COPY = mybir.ActivationFunctionType.Copy
+
+P = 128
+PACK = 4
+K, T, S, H, C, U = 512, 2048, 512, 512, 512, 1024
+HALF = S // 2
+LIST_COLS = HALF // 16
+FLOPS = 3 * 2 * K * H * S
+PAGE_CHUNKS = ((0, 512), (512, 768), (768, 1024))
+
+
+def words_view(dram):
+    return dram[0].rearrange("p n t -> p (n t)").bitcast(I32)
+
+
+def load_scale_rows(queue, tile, dram, first_row):
+    for q in range(4):
+        queue.dma_start(
+            out=tile[32 * q + first_row : 32 * q + first_row + 4, :].bitcast(I32),
+            in_=dram[0, 4 * q : 4 * q + 4, :].bitcast(I32),
+        )
+
+
+def deal_words(nc, dst, src):
+    nc.vector.tensor_copy(
+        out=dst.bitcast(I32).rearrange("p (t a i) -> p a t i", t=PACK, i=4),
+        in_=src.bitcast(I32).rearrange("p (a i t) -> p a t i", t=PACK, i=4),
+    )
+
+
+def deal_bytes(nc, dst, src):
+    nc.vector.tensor_copy(
+        out=dst.rearrange("p (t m) -> p t m", t=PACK),
+        in_=src.rearrange("p (m t) -> p t m", t=PACK),
+    )
+
+
+def tile_picked_twcmaxbpage_none_po_kernel(
+    tc, x_words, x_scales, w1_words, w1_scales, w2_words, w2_scales, gs, mem, offs, two, n1, n2, cand, n3, out_0, out_1, out_2
+):
+    nc = tc.nc
+    with ExitStack() as ctx:
+        keep = ctx.enter_context(tc.tile_pool(name="keep", bufs=1))
+        psum = ctx.enter_context(tc.psum_pool(name="psum", bufs=1))
+
+        def sb(name, shape, dtype, tag=None):
+            return keep.tile(shape, dtype, name=name, tag=tag or name, align_bytes=64)
+
+        def load_list(name, dram):
+            tile = sb(name, [P, S // 16], U16)
+            nc.sync.dma_start(tile[:], dram)
+            return tile
+
+        x_bytes = sb("x_bytes", [P, T], U8)
+        w_bytes = sb("w_bytes", [P, H], U8)
+        nc.vector.memset(x_bytes[:].bitcast(I32), 0)
+        nc.gpsimd.memset(w_bytes[:].bitcast(I32), 0)
+
+        w_raw = [sb(f"w_raw{i}", [P, H], U32) for i in range(2)]
+        nc.sync.dma_start(out=w_raw[0][:].bitcast(I32), in_=words_view(w1_words))
+        load_scale_rows(nc.sync, x_bytes, x_scales, 0)
+        offs_t = load_list("offs_t", offs)
+        x_table = sb("x_table", [P, T], U32)
+        nc.sync.dma_start(out=x_table[:].bitcast(I32), in_=words_view(x_words))
+        two_t = load_list("two_t", two)
+        load_scale_rows(nc.sync, w_bytes, w1_scales, 0)
+        load_scale_rows(nc.gpsimd, w_bytes, w2_scales, 4)
+        nc.sync.dma_start(out=w_raw[1][:].bitcast(I32), in_=words_view(w2_words))
+        n1_t = load_list("n1_t", n1)
+        n2_t = load_list("n2_t", n2)
+        cand_t = load_list("cand_t", cand)
+        gain = sb("gain", [P, PACK], F32)
+        nc.sync.dma_start(out=gain[:], in_=gs.rearrange("(p t) o -> p (t o)", t=PACK))
+        n3_t = load_list("n3_t", n3)
+        mem_rows = mem.rearrange("(p t) c -> p t c", t=PACK)
+        out_rows = out_0.rearrange("(p t) c -> p t c", t=PACK)
+
+        def pick(name, table, offsets, dtype, tag=None):
+            tile = sb(name, [P, S], dtype, tag)
+            nc.vector.tensor_copy(out=tile[:], in_=table[:].indirect(offsets[:]))
+            return tile
+
+        w_codes = [sb(f"w_codes{i}", [P, H], U32) for i in range(2)]
+        w_planes = sb("w_planes", [P, H], U8)
+        deal_words(nc, w_codes[0][:], w_raw[0][:])
+        offs_bytes = pick("offs_bytes", x_bytes, offs_t, U8)
+        two_bytes = pick("two_bytes", x_bytes, two_t, U8)
+        offs_words = pick("offs_words", x_table, offs_t, U32)
+        deal_words(nc, w_codes[1][:], w_raw[1][:])
+        deal_bytes(nc, w_planes[:], w_bytes[:])
+
+        def project(name, i, words, scale_bytes):
+            banks = [[psum.tile([P, 2, HALF], F32, name=f"{name}{h}{u}", tag=f"{name}{h}{u}") for u in range(2)] for h in range(2)]
+            rows = [sb(f"{name}_rows{t}", [P, S], F32) for t in range(PACK)]
+            for u in range(2):
+                for h in range(2):
+                    cols = slice(h * HALF, (h + 1) * HALF)
+                    for e in range(2):
+                        m = slice((2 * u + e) * P, (2 * u + e + 1) * P)
+                        nc.tensor.matmul_mx(
+                            out=banks[h][u][:, e, :],
+                            lhsT=w_codes[i][:, m].bitcast(FP8X4),
+                            lhsT_scale=w_planes[4 * i : P, m],
+                            rhs=words[:, cols].bitcast(FP8X4),
+                            rhs_scale=scale_bytes[:, cols],
+                            start=True,
+                            stop=True,
+                        )
+                for e in range(2):
+                    for h in range(2):
+                        nc.scalar.copy(out=rows[2 * u + e][:, h * HALF : (h + 1) * HALF], in_=banks[h][u][:, e, :])
+            return banks, rows
+
+        y_banks, y_rows = project("y", 0, offs_words, offs_bytes)
+        two_words = pick("two_words", x_table, two_t, U32)
+        d_banks, d_rows = project("d", 1, two_words, two_bytes)
+
+        cand_bytes = pick("cand_bytes", x_bytes, cand_t, U8, "w_bytes")
+        cand_words = pick("cand_words", x_table, cand_t, U32)
+        cand_codes = sb("cand_codes", [P, C], U32)
+        cand_plane = sb("cand_plane", [P, C], U8)
+        deal_words(nc, cand_codes[:], cand_words[:])
+        deal_bytes(nc, cand_plane[:], cand_bytes[:])
+
+        pages = [sb(f"page{t}", [P, U], F32, tag) for t, tag in enumerate(("w_bytes", "x_bytes", "x_table", "cand_words"))]
+        for t in range(PACK):
+            nc.sync.dma_start(out=pages[t][:], in_=mem_rows[:, t, :])
+
+        z_rows = [sb(f"z_rows{h}", [P, PACK, HALF], BF16) for h in range(2)]
+
+        def fetch(h, u):
+            cols = slice(h * LIST_COLS, (h + 1) * LIST_COLS)
+            y_at = sb(f"y_at{h}{u}", [P, 2, HALF], F32)
+            d_at = sb(f"d_at{h}{u}", [P, 2, HALF], F32)
+            for e in range(2):
+                nc.vector.tensor_copy(out=y_at[:, e, :], in_=y_rows[2 * u + e][:].indirect(n1_t[:, cols]))
+            for e in range(2):
+                nc.vector.tensor_copy(out=d_at[:, e, :], in_=d_rows[2 * u + e][:].indirect(n2_t[:, cols]))
+            return y_at, d_at
+
+        def extremes(h, u, y_at, d_at):
+            low = sb(f"low{h}{u}", [P, 2, HALF], F32)
+            high = sb(f"high{h}{u}", [P, 2, HALF], F32)
+            nc.vector.tensor_tensor(out=low[:], in0=y_at[:], in1=d_banks[h][u][:], op=ALU.min)
+            nc.vector.tensor_tensor(out=high[:], in0=d_at[:], in1=y_banks[h][u][:], op=ALU.max)
+            return low, high
+
+        def weigh(h, u, low, high):
+            gap = sb(f"gap{h}{u}", [P, 2, HALF], F32)
+            nc.vector.tensor_tensor(out=gap[:], in0=high[:], in1=low[:], op=ALU.subtract)
+            for e in range(2):
+                t = 2 * u + e
+                nc.scalar.activation(out=z_rows[h][:, t, :], in_=gap[:, e, :], func=COPY, scale=gain[:, t : t + 1])
+
+        def group(h):
+            z_grouped = sb(f"z_grouped{h}", [P, HALF, PACK], BF16)
+            nc.scalar.copy(out=z_grouped[:], in_=z_rows[h][:].rearrange("p t j -> p j t"))
+            return z_grouped
+
+        def score(h, z_grouped):
+            z_codes = sb(f"z_codes{h}", [P, HALF], U32)
+            z_plane = sb(f"z_plane{h}", [P, HALF], U8)
+            nc.vector.quantize_mx(out=z_codes[:].bitcast(FP8X4), scales=z_plane[:], in_=z_grouped[:].rearrange("p j t -> p (j t)"))
+            scores = sb(f"scores{h}", [P, PACK, HALF], F32)
+            for u in range(2):
+                bank = psum.tile([P, 2, HALF], F32, name=f"s{h}{u}", tag=f"d{h}{u}")
+                for e in range(2):
+                    m = slice((2 * u + e) * P, (2 * u + e + 1) * P)
+                    nc.tensor.matmul_mx(
+                        out=bank[:, e, :],
+                        lhsT=cand_codes[:, m].bitcast(FP8X4),
+                        lhsT_scale=cand_plane[:, m],
+                        rhs=z_codes[:].bitcast(FP8X4),
+                        rhs_scale=z_plane[:],
+                        start=True,
+                        stop=True,
+                    )
+                nc.scalar.activation(out=scores[:, 2 * u : 2 * u + 2, :], in_=bank[:], func=COPY, scale=0.0625)
+            return scores
+
+        def put(h, t, scores):
+            cols = slice(h * LIST_COLS, (h + 1) * LIST_COLS)
+            nc.vector.tensor_copy(out=pages[t][:].indirect(n3_t[:, cols]), in_=scores[:, t, :])
+
+        rounded = [sb(f"rounded{a}", [P, b - a, PACK], BF16) for a, b in PAGE_CHUNKS]
+        staged = [sb(f"staged{a}", [P, PACK, b - a], BF16) for a, b in PAGE_CHUNKS]
+
+        def store(t):
+            nc.sync.dma_start(out=out_rows[:, t, :], in_=pages[t][:])
+
+        def stage(engine_copy, t, chunks):
+            for c in chunks:
+                a, b = PAGE_CHUNKS[c]
+                engine_copy(out=staged[c][:, t, :], in_=pages[t][:, a:b])
+
+        def weave(engine_copy, c, first, last):
+            engine_copy(out=rounded[c][:, :, first:last], in_=staged[c][:, first:last, :].rearrange("p t c -> p c t"))
+
+        steps = [(h, u) for h in range(2) for u in range(2)]
+        pending = None
+        for h, u in steps:
+            fetched = fetch(h, u)
+            if pending is not None:
+                weigh(*pending)
+            if (h, u) == (1, 0):
+                z0 = group(0)
+            pending = (h, u) + extremes(h, u, *fetched)
+        scores0 = score(0, z0)
+        weigh(*pending)
+        z1 = group(1)
+        put(0, 0, scores0)
+        put(0, 1, scores0)
+        scores1 = score(1, z1)
+        put(0, 2, scores0)
+        for t in range(3):
+            put(1, t, scores1)
+            store(t)
+            stage(nc.scalar.copy, t, range(3))
+            if t == 1:
+                weave(nc.scalar.copy, 0, 0, 2)
+        for c in (1, 2):
+            weave(nc.scalar.copy, c, 0, 3)
+        put(0, 3, scores0)
+        put(1, 3, scores1)
+        store(3)
+        stage(nc.vector.tensor_copy, 3, (0,))
+        weave(nc.vector.tensor_copy, 0, 2, 4)
+        for c in (1, 2):
+            a, b = PAGE_CHUNKS[c]
+            nc.scalar.copy(out=rounded[c][:, :, 3], in_=pages[3][:, a:b])
+
+        out_words = words_view(out_1)
+        page_plane = sb("page_plane", [P, U], U8)
+        for c, (a, b) in enumerate(PAGE_CHUNKS):
+            codes = sb(f"page_codes{c}", [P, b - a], U32)
+            nc.vector.quantize_mx(out=codes[:].bitcast(FP8X4), scales=page_plane[:, a:b], in_=rounded[c][:].rearrange("p c t -> p (c t)"))
+            nc.sync.dma_start(out=out_words[:, a:b], in_=codes[:].bitcast(I32))
+        for q in range(4):
+            queue = nc.scalar if q % 2 == 0 else nc.sync
+            queue.dma_start(out=out_2[0, 4 * q : 4 * q + 4, :].bitcast(I32), in_=page_plane[32 * q : 32 * q + 4, :].bitcast(I32))

@@ -18,17 +18,17 @@ K, T, S, H, C, U = 512, 2048, 512, 512, 512, 1024
 HALF = S // 2
 LIST_COLS = HALF // 16
 FLOPS = 3 * 2 * K * H * S
-PAGE_CHUNKS = ((0, 512), (512, 768), (768, 1024))
+PAGE_CHUNKS = ((0, 256), (256, 512), (512, 768), (768, 1024))
 
 
 def words_view(dram):
     return dram[0].rearrange("p n t -> p (n t)").bitcast(I32)
 
 
-def load_scale_rows(queue, tile, dram, first_row):
+def load_scale_rows(queue, tile, dram):
     for q in range(4):
         queue.dma_start(
-            out=tile[32 * q + first_row : 32 * q + first_row + 4, :].bitcast(I32),
+            out=tile[32 * q : 32 * q + 4, :].bitcast(I32),
             in_=dram[0, 4 * q : 4 * q + 4, :].bitcast(I32),
         )
 
@@ -40,8 +40,8 @@ def deal_words(nc, dst, src):
     )
 
 
-def deal_bytes(nc, dst, src):
-    nc.vector.tensor_copy(
+def deal(engine, dst, src):
+    engine.tensor_copy(
         out=dst.rearrange("p (t m) -> p t m", t=PACK),
         in_=src.rearrange("p (m t) -> p t m", t=PACK),
     )
@@ -64,23 +64,25 @@ def tile_picked_twcmaxbpage_none_po_kernel(
             return tile
 
         x_bytes = sb("x_bytes", [P, T], U8)
-        w_bytes = sb("w_bytes", [P, H], U8)
-        nc.vector.memset(x_bytes[:].bitcast(I32), 0)
-        nc.gpsimd.memset(w_bytes[:].bitcast(I32), 0)
+        w_bytes = [sb(f"w_bytes{i}", [P, H], U8) for i in range(2)]
+        nc.vector.memset(x_bytes[:, : T // 2].bitcast(I32), 0)
+        nc.gpsimd.memset(x_bytes[:, T // 2 :].bitcast(I32), 0)
+        for i in range(2):
+            nc.gpsimd.memset(w_bytes[i][:].bitcast(I32), 0)
 
         w_raw = [sb(f"w_raw{i}", [P, H], U32) for i in range(2)]
-        nc.sync.dma_start(out=w_raw[0][:].bitcast(I32), in_=words_view(w1_words))
-        load_scale_rows(nc.sync, x_bytes, x_scales, 0)
         offs_t = load_list("offs_t", offs)
+        load_scale_rows(nc.sync, x_bytes, x_scales)
+        two_t = load_list("two_t", two)
+        nc.sync.dma_start(out=w_raw[0][:].bitcast(I32), in_=words_view(w1_words))
         x_table = sb("x_table", [P, T], U32)
         nc.sync.dma_start(out=x_table[:].bitcast(I32), in_=words_view(x_words))
-        two_t = load_list("two_t", two)
-        load_scale_rows(nc.sync, w_bytes, w1_scales, 0)
-        load_scale_rows(nc.gpsimd, w_bytes, w2_scales, 4)
+        load_scale_rows(nc.sync, w_bytes[0], w1_scales)
+        cand_t = load_list("cand_t", cand)
+        load_scale_rows(nc.sync, w_bytes[1], w2_scales)
         nc.sync.dma_start(out=w_raw[1][:].bitcast(I32), in_=words_view(w2_words))
         n1_t = load_list("n1_t", n1)
         n2_t = load_list("n2_t", n2)
-        cand_t = load_list("cand_t", cand)
         gain = sb("gain", [P, PACK], F32)
         nc.sync.dma_start(out=gain[:], in_=gs.rearrange("(p t) o -> p (t o)", t=PACK))
         n3_t = load_list("n3_t", n3)
@@ -93,13 +95,12 @@ def tile_picked_twcmaxbpage_none_po_kernel(
             return tile
 
         w_codes = [sb(f"w_codes{i}", [P, H], U32) for i in range(2)]
-        w_planes = sb("w_planes", [P, H], U8)
-        deal_words(nc, w_codes[0][:], w_raw[0][:])
+        w_planes = [sb(f"w_plane{i}", [P, H], U8) for i in range(2)]
+        deal(nc.gpsimd, w_codes[0][:].bitcast(I32), w_raw[0][:].bitcast(I32))
         offs_bytes = pick("offs_bytes", x_bytes, offs_t, U8)
         two_bytes = pick("two_bytes", x_bytes, two_t, U8)
         offs_words = pick("offs_words", x_table, offs_t, U32)
-        deal_words(nc, w_codes[1][:], w_raw[1][:])
-        deal_bytes(nc, w_planes[:], w_bytes[:])
+        deal(nc.gpsimd, w_planes[0][:], w_bytes[0][:])
 
         def project(name, i, words, scale_bytes):
             banks = [[psum.tile([P, 2, HALF], F32, name=f"{name}{h}{u}", tag=f"{name}{h}{u}") for u in range(2)] for h in range(2)]
@@ -112,7 +113,7 @@ def tile_picked_twcmaxbpage_none_po_kernel(
                         nc.tensor.matmul_mx(
                             out=banks[h][u][:, e, :],
                             lhsT=w_codes[i][:, m].bitcast(FP8X4),
-                            lhsT_scale=w_planes[4 * i : P, m],
+                            lhsT_scale=w_planes[i][:, m],
                             rhs=words[:, cols].bitcast(FP8X4),
                             rhs_scale=scale_bytes[:, cols],
                             start=True,
@@ -125,16 +126,18 @@ def tile_picked_twcmaxbpage_none_po_kernel(
 
         y_banks, y_rows = project("y", 0, offs_words, offs_bytes)
         two_words = pick("two_words", x_table, two_t, U32)
+        deal(nc.gpsimd, w_codes[1][:].bitcast(I32), w_raw[1][:].bitcast(I32))
+        deal(nc.gpsimd, w_planes[1][:], w_bytes[1][:])
         d_banks, d_rows = project("d", 1, two_words, two_bytes)
 
-        cand_bytes = pick("cand_bytes", x_bytes, cand_t, U8, "w_bytes")
+        cand_bytes = pick("cand_bytes", x_bytes, cand_t, U8)
         cand_words = pick("cand_words", x_table, cand_t, U32)
         cand_codes = sb("cand_codes", [P, C], U32)
         cand_plane = sb("cand_plane", [P, C], U8)
         deal_words(nc, cand_codes[:], cand_words[:])
-        deal_bytes(nc, cand_plane[:], cand_bytes[:])
+        deal(nc.vector, cand_plane[:], cand_bytes[:])
 
-        pages = [sb(f"page{t}", [P, U], F32, tag) for t, tag in enumerate(("w_bytes", "x_bytes", "x_table", "cand_words"))]
+        pages = [sb(f"page{t}", [P, U], F32, tag) for t, tag in enumerate(("w_bytes1", "x_bytes", "x_table", "cand_words"))]
         for t in range(PACK):
             nc.sync.dma_start(out=pages[t][:], in_=mem_rows[:, t, :])
 
@@ -143,7 +146,7 @@ def tile_picked_twcmaxbpage_none_po_kernel(
         def fetch(h, u):
             cols = slice(h * LIST_COLS, (h + 1) * LIST_COLS)
             y_at = sb(f"y_at{h}{u}", [P, 2, HALF], F32)
-            d_at = sb(f"d_at{h}{u}", [P, 2, HALF], F32)
+            d_at = sb(f"d_at{h}{u}", [P, 2, HALF], F32, "z_grouped0" if (h, u) == (1, 1) else None)
             for e in range(2):
                 nc.vector.tensor_copy(out=y_at[:, e, :], in_=y_rows[2 * u + e][:].indirect(n1_t[:, cols]))
             for e in range(2):
@@ -159,7 +162,8 @@ def tile_picked_twcmaxbpage_none_po_kernel(
 
         def weigh(h, u, low, high):
             gap = sb(f"gap{h}{u}", [P, 2, HALF], F32)
-            nc.vector.tensor_tensor(out=gap[:], in0=high[:], in1=low[:], op=ALU.subtract)
+            engine = nc.vector if (h, u) == (1, 1) else nc.gpsimd
+            engine.tensor_tensor(out=gap[:], in0=high[:], in1=low[:], op=ALU.subtract)
             for e in range(2):
                 t = 2 * u + e
                 nc.scalar.activation(out=z_rows[h][:, t, :], in_=gap[:, e, :], func=COPY, scale=gain[:, t : t + 1])
@@ -173,7 +177,7 @@ def tile_picked_twcmaxbpage_none_po_kernel(
             z_codes = sb(f"z_codes{h}", [P, HALF], U32)
             z_plane = sb(f"z_plane{h}", [P, HALF], U8)
             nc.vector.quantize_mx(out=z_codes[:].bitcast(FP8X4), scales=z_plane[:], in_=z_grouped[:].rearrange("p j t -> p (j t)"))
-            scores = sb(f"scores{h}", [P, PACK, HALF], F32)
+            banks = []
             for u in range(2):
                 bank = psum.tile([P, 2, HALF], F32, name=f"s{h}{u}", tag=f"d{h}{u}")
                 for e in range(2):
@@ -187,23 +191,25 @@ def tile_picked_twcmaxbpage_none_po_kernel(
                         start=True,
                         stop=True,
                     )
-                nc.scalar.activation(out=scores[:, 2 * u : 2 * u + 2, :], in_=bank[:], func=COPY, scale=0.0625)
-            return scores
+                banks.append(bank)
+            return banks
+
+        def scale_out(dst, src):
+            nc.scalar.activation(out=dst, in_=src, func=COPY, scale=0.0625)
 
         def put(h, t, scores):
             cols = slice(h * LIST_COLS, (h + 1) * LIST_COLS)
-            nc.vector.tensor_copy(out=pages[t][:].indirect(n3_t[:, cols]), in_=scores[:, t, :])
+            nc.vector.tensor_copy(out=pages[t][:].indirect(n3_t[:, cols]), in_=scores)
 
         rounded = [sb(f"rounded{a}", [P, b - a, PACK], BF16) for a, b in PAGE_CHUNKS]
-        staged = [sb(f"staged{a}", [P, PACK, b - a], BF16) for a, b in PAGE_CHUNKS]
+        staged = [sb(f"staged{c}", [P, PACK, b - a], BF16) for c, (a, b) in enumerate(PAGE_CHUNKS)]
 
         def store(t):
             nc.sync.dma_start(out=out_rows[:, t, :], in_=pages[t][:])
 
-        def stage(engine_copy, t, chunks):
-            for c in chunks:
-                a, b = PAGE_CHUNKS[c]
-                engine_copy(out=staged[c][:, t, :], in_=pages[t][:, a:b])
+        def stage(engine_copy, t, c):
+            a, b = PAGE_CHUNKS[c]
+            engine_copy(out=staged[c][:, t, :], in_=pages[t][:, a:b])
 
         def weave(engine_copy, c, first, last):
             engine_copy(out=rounded[c][:, :, first:last], in_=staged[c][:, first:last, :].rearrange("p t c -> p c t"))
@@ -211,39 +217,54 @@ def tile_picked_twcmaxbpage_none_po_kernel(
         steps = [(h, u) for h in range(2) for u in range(2)]
         pending = None
         for h, u in steps:
+            if (h, u) == (1, 1):
+                banks0 = score(0, z0)
             fetched = fetch(h, u)
             if pending is not None:
                 weigh(*pending)
             if (h, u) == (1, 0):
                 z0 = group(0)
             pending = (h, u) + extremes(h, u, *fetched)
-        scores0 = score(0, z0)
+        first0 = sb("first0", [P, 2, HALF], F32)
+        last = sb("last", [P, S], F32)
+        scale_out(first0[:], banks0[0][:])
+        scale_out(last[:, :HALF], banks0[1][:, 1, :])
         weigh(*pending)
+        put(0, 0, first0[:, 0, :])
         z1 = group(1)
-        put(0, 0, scores0)
-        put(0, 1, scores0)
-        scores1 = score(1, z1)
-        put(0, 2, scores0)
+        third0 = sb("third0", [P, HALF], F32, "z_rows1")
+        scale_out(third0[:], banks0[1][:, 0, :])
+        put(0, 1, first0[:, 1, :])
+        banks1 = score(1, z1)
+        put(0, 2, third0[:])
+        scores1 = sb("scores1", [P, 3, HALF], F32)
         for t in range(3):
-            put(1, t, scores1)
+            scale_out(scores1[:, t, :], banks1[t // 2][:, t % 2, :])
+        scale_out(last[:, HALF:], banks1[1][:, 1, :])
+        for t in range(3):
+            put(1, t, scores1[:, t, :])
             store(t)
-            stage(nc.scalar.copy, t, range(3))
+            for c in range(4):
+                stage(nc.scalar.copy, t, c)
             if t == 1:
-                weave(nc.scalar.copy, 0, 0, 2)
-        for c in (1, 2):
+                for c in (0, 1):
+                    weave(nc.scalar.copy, c, 0, 2)
+        for c in (2, 3):
             weave(nc.scalar.copy, c, 0, 3)
-        put(0, 3, scores0)
-        put(1, 3, scores1)
+        nc.vector.tensor_copy(out=pages[3][:].indirect(n3_t[:]), in_=last[:])
         store(3)
-        stage(nc.vector.tensor_copy, 3, (0,))
-        weave(nc.vector.tensor_copy, 0, 2, 4)
-        for c in (1, 2):
+        for c in (0, 1):
+            stage(nc.vector.tensor_copy, 3, c)
+        for c in (0, 1):
+            weave(nc.vector.tensor_copy, c, 2, 4)
+        for c in (2, 3):
             a, b = PAGE_CHUNKS[c]
             nc.scalar.copy(out=rounded[c][:, :, 3], in_=pages[3][:, a:b])
 
         out_words = words_view(out_1)
         page_plane = sb("page_plane", [P, U], U8)
-        for c, (a, b) in enumerate(PAGE_CHUNKS):
+        for c in (0, 2, 1, 3):
+            a, b = PAGE_CHUNKS[c]
             codes = sb(f"page_codes{c}", [P, b - a], U32)
             nc.vector.quantize_mx(out=codes[:].bitcast(FP8X4), scales=page_plane[:, a:b], in_=rounded[c][:].rearrange("p c t -> p (c t)"))
             nc.sync.dma_start(out=out_words[:, a:b], in_=codes[:].bitcast(I32))

@@ -25,9 +25,9 @@ def words_view(dram):
     return dram[0].rearrange("p n t -> p (n t)").bitcast(I32)
 
 
-def load_scale_rows(queue, tile, dram):
+def load_scale_rows(queues, tile, dram):
     for q in range(4):
-        queue.dma_start(
+        queues[q % len(queues)].dma_start(
             out=tile[32 * q : 32 * q + 4, :].bitcast(I32),
             in_=dram[0, 4 * q : 4 * q + 4, :].bitcast(I32),
         )
@@ -72,14 +72,14 @@ def tile_picked_twcmaxbpage_none_po_kernel(
 
         w_raw = [sb(f"w_raw{i}", [P, H], U32) for i in range(2)]
         offs_t = load_list("offs_t", offs)
-        load_scale_rows(nc.sync, x_bytes, x_scales)
+        load_scale_rows((nc.scalar, nc.sync), x_bytes, x_scales)
         two_t = load_list("two_t", two)
         nc.sync.dma_start(out=w_raw[0][:].bitcast(I32), in_=words_view(w1_words))
         x_table = sb("x_table", [P, T], U32)
         nc.sync.dma_start(out=x_table[:].bitcast(I32), in_=words_view(x_words))
-        load_scale_rows(nc.sync, w_bytes[0], w1_scales)
+        load_scale_rows((nc.sync,), w_bytes[0], w1_scales)
         cand_t = load_list("cand_t", cand)
-        load_scale_rows(nc.sync, w_bytes[1], w2_scales)
+        load_scale_rows((nc.sync,), w_bytes[1], w2_scales)
         nc.sync.dma_start(out=w_raw[1][:].bitcast(I32), in_=words_view(w2_words))
         n1_t = load_list("n1_t", n1)
         n2_t = load_list("n2_t", n2)
@@ -141,12 +141,12 @@ def tile_picked_twcmaxbpage_none_po_kernel(
         for t in range(PACK):
             nc.sync.dma_start(out=pages[t][:], in_=mem_rows[:, t, :])
 
-        z_rows = [sb(f"z_rows{h}", [P, PACK, HALF], BF16) for h in range(2)]
+        z_rows = [sb(f"z_rows{h}", [P, PACK, HALF], BF16, "z_rows") for h in range(2)]
 
         def fetch(h, u):
             cols = slice(h * LIST_COLS, (h + 1) * LIST_COLS)
-            y_at = sb(f"y_at{h}{u}", [P, 2, HALF], F32)
-            d_at = sb(f"d_at{h}{u}", [P, 2, HALF], F32, "z_grouped0" if (h, u) == (1, 1) else None)
+            y_at = sb(f"y_at{h}{u}", [P, 2, HALF], F32, "y_at")
+            d_at = sb(f"d_at{h}{u}", [P, 2, HALF], F32, "d_at")
             for e in range(2):
                 nc.vector.tensor_copy(out=y_at[:, e, :], in_=y_rows[2 * u + e][:].indirect(n1_t[:, cols]))
             for e in range(2):
@@ -154,16 +154,16 @@ def tile_picked_twcmaxbpage_none_po_kernel(
             return y_at, d_at
 
         def extremes(h, u, y_at, d_at):
-            low = sb(f"low{h}{u}", [P, 2, HALF], F32)
-            high = sb(f"high{h}{u}", [P, 2, HALF], F32)
-            nc.vector.tensor_tensor(out=low[:], in0=y_at[:], in1=d_banks[h][u][:], op=ALU.min)
-            nc.vector.tensor_tensor(out=high[:], in0=d_at[:], in1=y_banks[h][u][:], op=ALU.max)
+            ends = sb(f"ends{h}{u}", [P, 2, 2, HALF], F32, "z_grouped0" if (h, u) == (1, 1) else None)
+            low, high = ends[:, 0], ends[:, 1]
+            nc.vector.tensor_tensor(out=low, in0=y_at[:], in1=d_banks[h][u][:], op=ALU.min)
+            nc.vector.tensor_tensor(out=high, in0=d_at[:], in1=y_banks[h][u][:], op=ALU.max)
             return low, high
 
         def weigh(h, u, low, high):
             gap = sb(f"gap{h}{u}", [P, 2, HALF], F32)
             engine = nc.vector if (h, u) == (1, 1) else nc.gpsimd
-            engine.tensor_tensor(out=gap[:], in0=high[:], in1=low[:], op=ALU.subtract)
+            engine.tensor_tensor(out=gap[:], in0=high, in1=low, op=ALU.subtract)
             for e in range(2):
                 t = 2 * u + e
                 nc.scalar.activation(out=z_rows[h][:, t, :], in_=gap[:, e, :], func=COPY, scale=gain[:, t : t + 1])
@@ -217,22 +217,23 @@ def tile_picked_twcmaxbpage_none_po_kernel(
         steps = [(h, u) for h in range(2) for u in range(2)]
         pending = None
         for h, u in steps:
+            fetched = fetch(h, u)
             if (h, u) == (1, 1):
                 banks0 = score(0, z0)
-            fetched = fetch(h, u)
             if pending is not None:
                 weigh(*pending)
             if (h, u) == (1, 0):
                 z0 = group(0)
             pending = (h, u) + extremes(h, u, *fetched)
-        first0 = sb("first0", [P, 2, HALF], F32)
+        first0 = sb("first0", [P, 2, HALF], F32, "d_at")
         last = sb("last", [P, S], F32)
-        scale_out(first0[:], banks0[0][:])
+        for t in range(2):
+            scale_out(first0[:, t, :], banks0[0][:, t, :])
         scale_out(last[:, :HALF], banks0[1][:, 1, :])
         weigh(*pending)
         put(0, 0, first0[:, 0, :])
         z1 = group(1)
-        third0 = sb("third0", [P, HALF], F32, "z_rows1")
+        third0 = sb("third0", [P, HALF], F32, "z_rows")
         scale_out(third0[:], banks0[1][:, 0, :])
         put(0, 1, first0[:, 1, :])
         banks1 = score(1, z1)

@@ -71,16 +71,16 @@ def tile_picked_twcmaxbpage_none_po_kernel(
             nc.gpsimd.memset(w_bytes[i][:].bitcast(I32), 0)
 
         w_raw = [sb(f"w_raw{i}", [P, H], U32) for i in range(2)]
+        nc.sync.dma_start(out=w_raw[0][:].bitcast(I32), in_=words_view(w1_words))
         offs_t = load_list("offs_t", offs)
         load_scale_rows((nc.scalar, nc.sync), x_bytes, x_scales)
         two_t = load_list("two_t", two)
-        nc.sync.dma_start(out=w_raw[0][:].bitcast(I32), in_=words_view(w1_words))
         x_table = sb("x_table", [P, T], U32)
         nc.sync.dma_start(out=x_table[:].bitcast(I32), in_=words_view(x_words))
         load_scale_rows((nc.sync,), w_bytes[0], w1_scales)
+        nc.sync.dma_start(out=w_raw[1][:].bitcast(I32), in_=words_view(w2_words))
         cand_t = load_list("cand_t", cand)
         load_scale_rows((nc.sync,), w_bytes[1], w2_scales)
-        nc.sync.dma_start(out=w_raw[1][:].bitcast(I32), in_=words_view(w2_words))
         n1_t = load_list("n1_t", n1)
         n2_t = load_list("n2_t", n2)
         gain = sb("gain", [P, PACK], F32)
@@ -96,7 +96,7 @@ def tile_picked_twcmaxbpage_none_po_kernel(
 
         w_codes = [sb(f"w_codes{i}", [P, H], U32) for i in range(2)]
         w_planes = [sb(f"w_plane{i}", [P, H], U8) for i in range(2)]
-        deal(nc.gpsimd, w_codes[0][:].bitcast(I32), w_raw[0][:].bitcast(I32))
+        deal_words(nc, w_codes[0][:], w_raw[0][:])
         offs_bytes = pick("offs_bytes", x_bytes, offs_t, U8)
         two_bytes = pick("two_bytes", x_bytes, two_t, U8)
         offs_words = pick("offs_words", x_table, offs_t, U32)
@@ -126,7 +126,7 @@ def tile_picked_twcmaxbpage_none_po_kernel(
 
         y_banks, y_rows = project("y", 0, offs_words, offs_bytes)
         two_words = pick("two_words", x_table, two_t, U32)
-        deal(nc.gpsimd, w_codes[1][:].bitcast(I32), w_raw[1][:].bitcast(I32))
+        deal_words(nc, w_codes[1][:], w_raw[1][:])
         deal(nc.gpsimd, w_planes[1][:], w_bytes[1][:])
         d_banks, d_rows = project("d", 1, two_words, two_bytes)
 

from contextlib import ExitStack

import concourse.mybir as mybir

F32 = mybir.dt.float32
BF16 = mybir.dt.bfloat16
I32 = mybir.dt.int32
U32 = mybir.dt.uint32
U16 = mybir.dt.uint16
U8 = mybir.dt.uint8
FP8X4 = mybir.dt.float8_e4m3fn_x4
ALU = mybir.AluOpType
COPY = mybir.ActivationFunctionType.Copy

P = 128
PACK = 4
K, T, S, H, C, U = 512, 2048, 512, 512, 512, 1024
HALF = S // 2
LIST_COLS = HALF // 16
FLOPS = 3 * 2 * K * H * S
PAGE_CHUNKS = ((0, 256), (256, 512), (512, 768), (768, 1024))


def words_view(dram):
    return dram[0].rearrange("p n t -> p (n t)").bitcast(I32)


def load_scale_rows(queues, tile, dram):
    for q in range(4):
        queues[q % len(queues)].dma_start(
            out=tile[32 * q : 32 * q + 4, :].bitcast(I32),
            in_=dram[0, 4 * q : 4 * q + 4, :].bitcast(I32),
        )


def deal_words(nc, dst, src):
    nc.vector.tensor_copy(
        out=dst.bitcast(I32).rearrange("p (t a i) -> p a t i", t=PACK, i=4),
        in_=src.bitcast(I32).rearrange("p (a i t) -> p a t i", t=PACK, i=4),
    )


def deal(engine, dst, src):
    engine.tensor_copy(
        out=dst.rearrange("p (t m) -> p t m", t=PACK),
        in_=src.rearrange("p (m t) -> p t m", t=PACK),
    )


def tile_picked_twcmaxbpage_none_po_kernel(
    tc, x_words, x_scales, w1_words, w1_scales, w2_words, w2_scales, gs, mem, offs, two, n1, n2, cand, n3, out_0, out_1, out_2
):
    nc = tc.nc
    with ExitStack() as ctx:
        keep = ctx.enter_context(tc.tile_pool(name="keep", bufs=1))
        psum = ctx.enter_context(tc.psum_pool(name="psum", bufs=1))

        def sb(name, shape, dtype, tag=None):
            return keep.tile(shape, dtype, name=name, tag=tag or name, align_bytes=64)

        def load_list(name, dram):
            tile = sb(name, [P, S // 16], U16)
            nc.sync.dma_start(tile[:], dram)
            return tile

        x_bytes = sb("x_bytes", [P, T], U8)
        w_bytes = [sb(f"w_bytes{i}", [P, H], U8) for i in range(2)]
        nc.vector.memset(x_bytes[:, : T // 2].bitcast(I32), 0)
        nc.gpsimd.memset(x_bytes[:, T // 2 :].bitcast(I32), 0)
        for i in range(2):
            nc.gpsimd.memset(w_bytes[i][:].bitcast(I32), 0)

        w_raw = [sb(f"w_raw{i}", [P, H], U32) for i in range(2)]
        nc.sync.dma_start(out=w_raw[0][:].bitcast(I32), in_=words_view(w1_words))
        offs_t = load_list("offs_t", offs)
        load_scale_rows((nc.scalar, nc.sync), x_bytes, x_scales)
        two_t = load_list("two_t", two)
        x_table = sb("x_table", [P, T], U32)
        nc.sync.dma_start(out=x_table[:].bitcast(I32), in_=words_view(x_words))
        load_scale_rows((nc.sync,), w_bytes[0], w1_scales)
        nc.sync.dma_start(out=w_raw[1][:].bitcast(I32), in_=words_view(w2_words))
        cand_t = load_list("cand_t", cand)
        load_scale_rows((nc.sync,), w_bytes[1], w2_scales)
        n1_t = load_list("n1_t", n1)
        n2_t = load_list("n2_t", n2)
        gain = sb("gain", [P, PACK], F32)
        nc.sync.dma_start(out=gain[:], in_=gs.rearrange("(p t) o -> p (t o)", t=PACK))
        n3_t = load_list("n3_t", n3)
        mem_rows = mem.rearrange("(p t) c -> p t c", t=PACK)
        out_rows = out_0.rearrange("(p t) c -> p t c", t=PACK)

        def pick(name, table, offsets, dtype, tag=None):
            tile = sb(name, [P, S], dtype, tag)
            nc.vector.tensor_copy(out=tile[:], in_=table[:].indirect(offsets[:]))
            return tile

        w_codes = [sb(f"w_codes{i}", [P, H], U32) for i in range(2)]
        w_planes = [sb(f"w_plane{i}", [P, H], U8) for i in range(2)]
        deal_words(nc, w_codes[0][:], w_raw[0][:])
        offs_bytes = pick("offs_bytes", x_bytes, offs_t, U8)
        two_bytes = pick("two_bytes", x_bytes, two_t, U8)
        offs_words = pick("offs_words", x_table, offs_t, U32)
        deal(nc.gpsimd, w_planes[0][:], w_bytes[0][:])

        def project(name, i, words, scale_bytes):
            banks = [[psum.tile([P, 2, HALF], F32, name=f"{name}{h}{u}", tag=f"{name}{h}{u}") for u in range(2)] for h in range(2)]
            rows = [sb(f"{name}_rows{t}", [P, S], F32) for t in range(PACK)]
            for u in range(2):
                for h in range(2):
                    cols = slice(h * HALF, (h + 1) * HALF)
                    for e in range(2):
                        m = slice((2 * u + e) * P, (2 * u + e + 1) * P)
                        nc.tensor.matmul_mx(
                            out=banks[h][u][:, e, :],
                            lhsT=w_codes[i][:, m].bitcast(FP8X4),
                            lhsT_scale=w_planes[i][:, m],
                            rhs=words[:, cols].bitcast(FP8X4),
                            rhs_scale=scale_bytes[:, cols],
                            start=True,
                            stop=True,
                        )
                for e in range(2):
                    for h in range(2):
                        nc.scalar.copy(out=rows[2 * u + e][:, h * HALF : (h + 1) * HALF], in_=banks[h][u][:, e, :])
            return banks, rows

        y_banks, y_rows = project("y", 0, offs_words, offs_bytes)
        two_words = pick("two_words", x_table, two_t, U32)
        deal_words(nc, w_codes[1][:], w_raw[1][:])
        deal(nc.gpsimd, w_planes[1][:], w_bytes[1][:])
        d_banks, d_rows = project("d", 1, two_words, two_bytes)

        cand_bytes = pick("cand_bytes", x_bytes, cand_t, U8)
        cand_words = pick("cand_words", x_table, cand_t, U32)
        cand_codes = sb("cand_codes", [P, C], U32)
        cand_plane = sb("cand_plane", [P, C], U8)
        deal_words(nc, cand_codes[:], cand_words[:])
        deal(nc.vector, cand_plane[:], cand_bytes[:])

        pages = [sb(f"page{t}", [P, U], F32, tag) for t, tag in enumerate(("w_bytes1", "x_bytes", "x_table", "cand_words"))]
        for t in range(PACK):
            nc.sync.dma_start(out=pages[t][:], in_=mem_rows[:, t, :])

        z_rows = [sb(f"z_rows{h}", [P, PACK, HALF], BF16, "z_rows") for h in range(2)]

        def fetch(h, u):
            cols = slice(h * LIST_COLS, (h + 1) * LIST_COLS)
            y_at = sb(f"y_at{h}{u}", [P, 2, HALF], F32, "y_at")
            d_at = sb(f"d_at{h}{u}", [P, 2, HALF], F32, "d_at")
            for e in range(2):
                nc.vector.tensor_copy(out=y_at[:, e, :], in_=y_rows[2 * u + e][:].indirect(n1_t[:, cols]))
            for e in range(2):
                nc.vector.tensor_copy(out=d_at[:, e, :], in_=d_rows[2 * u + e][:].indirect(n2_t[:, cols]))
            return y_at, d_at

        def extremes(h, u, y_at, d_at):
            ends = sb(f"ends{h}{u}", [P, 2, 2, HALF], F32, "z_grouped0" if (h, u) == (1, 1) else None)
            low, high = ends[:, 0], ends[:, 1]
            nc.vector.tensor_tensor(out=low, in0=y_at[:], in1=d_banks[h][u][:], op=ALU.min)
            nc.vector.tensor_tensor(out=high, in0=d_at[:], in1=y_banks[h][u][:], op=ALU.max)
            return low, high

        def weigh(h, u, low, high):
            gap = sb(f"gap{h}{u}", [P, 2, HALF], F32)
            engine = nc.vector if (h, u) == (1, 1) else nc.gpsimd
            engine.tensor_tensor(out=gap[:], in0=high, in1=low, op=ALU.subtract)
            for e in range(2):
                t = 2 * u + e
                nc.scalar.activation(out=z_rows[h][:, t, :], in_=gap[:, e, :], func=COPY, scale=gain[:, t : t + 1])

        def group(h):
            z_grouped = sb(f"z_grouped{h}", [P, HALF, PACK], BF16)
            nc.scalar.copy(out=z_grouped[:], in_=z_rows[h][:].rearrange("p t j -> p j t"))
            return z_grouped

        def score(h, z_grouped):
            z_codes = sb(f"z_codes{h}", [P, HALF], U32)
            z_plane = sb(f"z_plane{h}", [P, HALF], U8)
            nc.vector.quantize_mx(out=z_codes[:].bitcast(FP8X4), scales=z_plane[:], in_=z_grouped[:].rearrange("p j t -> p (j t)"))
            banks = []
            for u in range(2):
                bank = psum.tile([P, 2, HALF], F32, name=f"s{h}{u}", tag=f"d{h}{u}")
                for e in range(2):
                    m = slice((2 * u + e) * P, (2 * u + e + 1) * P)
                    nc.tensor.matmul_mx(
                        out=bank[:, e, :],
                        lhsT=cand_codes[:, m].bitcast(FP8X4),
                        lhsT_scale=cand_plane[:, m],
                        rhs=z_codes[:].bitcast(FP8X4),
                        rhs_scale=z_plane[:],
                        start=True,
                        stop=True,
                    )
                banks.append(bank)
            return banks

        def scale_out(dst, src):
            nc.scalar.activation(out=dst, in_=src, func=COPY, scale=0.0625)

        def put(h, t, scores):
            cols = slice(h * LIST_COLS, (h + 1) * LIST_COLS)
            nc.vector.tensor_copy(out=pages[t][:].indirect(n3_t[:, cols]), in_=scores)

        rounded = [sb(f"rounded{a}", [P, b - a, PACK], BF16) for a, b in PAGE_CHUNKS]
        staged = [sb(f"staged{c}", [P, PACK, b - a], BF16) for c, (a, b) in enumerate(PAGE_CHUNKS)]

        def store(t):
            nc.sync.dma_start(out=out_rows[:, t, :], in_=pages[t][:])

        def stage(engine_copy, t, c):
            a, b = PAGE_CHUNKS[c]
            engine_copy(out=staged[c][:, t, :], in_=pages[t][:, a:b])

        def weave(engine_copy, c, first, last):
            engine_copy(out=rounded[c][:, :, first:last], in_=staged[c][:, first:last, :].rearrange("p t c -> p c t"))

        steps = [(h, u) for h in range(2) for u in range(2)]
        pending = None
        for h, u in steps:
            fetched = fetch(h, u)
            if (h, u) == (1, 1):
                banks0 = score(0, z0)
            if pending is not None:
                weigh(*pending)
            if (h, u) == (1, 0):
                z0 = group(0)
            pending = (h, u) + extremes(h, u, *fetched)
        first0 = sb("first0", [P, 2, HALF], F32, "d_at")
        last = sb("last", [P, S], F32)
        for t in range(2):
            scale_out(first0[:, t, :], banks0[0][:, t, :])
        scale_out(last[:, :HALF], banks0[1][:, 1, :])
        weigh(*pending)
        put(0, 0, first0[:, 0, :])
        z1 = group(1)
        third0 = sb("third0", [P, HALF], F32, "z_rows")
        scale_out(third0[:], banks0[1][:, 0, :])
        put(0, 1, first0[:, 1, :])
        banks1 = score(1, z1)
        put(0, 2, third0[:])
        scores1 = sb("scores1", [P, 3, HALF], F32)
        for t in range(3):
            scale_out(scores1[:, t, :], banks1[t // 2][:, t % 2, :])
        scale_out(last[:, HALF:], banks1[1][:, 1, :])
        for t in range(3):
            put(1, t, scores1[:, t, :])
            store(t)
            for c in range(4):
                stage(nc.scalar.copy, t, c)
            if t == 1:
                for c in (0, 1):
                    weave(nc.scalar.copy, c, 0, 2)
        for c in (2, 3):
            weave(nc.scalar.copy, c, 0, 3)
        nc.vector.tensor_copy(out=pages[3][:].indirect(n3_t[:]), in_=last[:])
        store(3)
        for c in (0, 1):
            stage(nc.vector.tensor_copy, 3, c)
        for c in (0, 1):
            weave(nc.vector.tensor_copy, c, 2, 4)
        for c in (2, 3):
            a, b = PAGE_CHUNKS[c]
            nc.scalar.copy(out=rounded[c][:, :, 3], in_=pages[3][:, a:b])

        out_words = words_view(out_1)
        page_plane = sb("page_plane", [P, U], U8)
        for c in (0, 2, 1, 3):
            a, b = PAGE_CHUNKS[c]
            codes = sb(f"page_codes{c}", [P, b - a], U32)
            nc.vector.quantize_mx(out=codes[:].bitcast(FP8X4), scales=page_plane[:, a:b], in_=rounded[c][:].rearrange("p c t -> p (c t)"))
            nc.sync.dma_start(out=out_words[:, a:b], in_=codes[:].bitcast(I32))
        for q in range(4):
            queue = nc.scalar if q % 2 == 0 else nc.sync
            queue.dma_start(out=out_2[0, 4 * q : 4 * q + 4, :].bitcast(I32), in_=page_plane[32 * q : 32 * q + 4, :].bitcast(I32))
